import numpy as np
import ml_dtypes


def mxq(x, axis, fmt="e4m3"):
    dtype, down = {"e4m3": (ml_dtypes.float8_e4m3fn, 7), "e5m2": (ml_dtypes.float8_e5m2, 14)}[fmt]
    v = np.moveaxis(np.asarray(x, np.float32).astype(ml_dtypes.bfloat16).astype(np.float64), axis, -1)
    blocks = v.reshape(v.shape[:-1] + (-1, 32))
    amax = np.abs(blocks).max(-1, keepdims=True)
    byte = np.maximum(np.where(amax > 0, np.frexp(amax)[1] - 1 + 127, 0) - down, 1)
    scale = np.exp2(byte - 127.0)
    codes = (blocks / scale).astype(np.float32).astype(dtype).astype(np.float64)
    return np.moveaxis((codes * scale).reshape(v.shape), -1, axis)


WIDE = False


def mx_kscale(k):
    if not WIDE:
        return np.ones(k)
    levels = np.array([10, -10, 5, -5, 0])
    if k % 512:
        return np.exp2(np.random.permutation(np.resize(levels, k // 32))).repeat(32)
    a = np.empty((k // 512, 16))
    for p in range(k // 512):
        a[p, :8] = np.random.permutation(np.resize(levels, 8))
        for g in range(8):
            far = levels[np.abs(levels - a[p, g]) >= 10]
            a[p, g + 8] = far[np.random.randint(len(far))]
    return np.exp2(a.ravel()).repeat(32)


def f64(x):
    return np.asarray(x).astype(np.float64)


def striped(idx):
    return np.tile(np.asarray(idx).reshape(-1, 16).T, (8, 1)).astype(np.uint16)


def unstriped(offs):
    return offs[:16].T.reshape(-1).astype(np.int64)


E2M1 = np.array([0.0, 0.5, 1.0, 1.5, 2.0, 3.0, 4.0, 6.0, -0.0, -0.5, -1.0, -1.5, -2.0, -3.0, -4.0, -6.0])


def pack_weight(w, fmt):
    k, n = w.shape
    w = f64(np.asarray(w, np.float32).astype(ml_dtypes.bfloat16)).reshape(k // 32, 32, n)
    amax = np.abs(w).max(1)
    if fmt == "e4m3":
        byte = np.frexp(amax)[1] - 1 + 127 - 7
    else:
        mant, ex = np.frexp(amax / 6.0)
        byte = np.where(mant > 0.5, ex, ex - 1) + 127
    byte = np.clip(np.where(amax > 0, byte, 1), 1, 254)
    scaled = (w * np.exp2(127.0 - byte)[:, None, :]).reshape(k, n).astype(np.float32)
    by_word = np.ascontiguousarray(scaled.reshape(k // 512, 128, 4, n).transpose(0, 1, 3, 2))
    if fmt == "e4m3":
        words = by_word.astype(ml_dtypes.float8_e4m3fn).view(np.uint8)
    else:
        c = by_word.astype(ml_dtypes.float4_e2m1fn).view(np.uint8) & 0xF
        words = (c[..., 0::2] | (c[..., 1::2] << 4)).reshape(k // 512, 128, 2 * n)
    return np.ascontiguousarray(words), np.ascontiguousarray(byte.astype(np.uint8).reshape(k // 512, 16, n))


def unpack_weight(words, scales, fmt):
    g, _, n = scales.shape
    words = np.ascontiguousarray(words).reshape(g, 128, n, -1)
    if fmt == "e4m3":
        vals = words.view(ml_dtypes.float8_e4m3fn).astype(np.float64)
    else:
        nib = np.empty((g, 128, n, 4), np.uint8)
        nib[..., 0::2] = words & 0xF
        nib[..., 1::2] = words >> 4
        vals = E2M1[nib]
    vals = vals * np.repeat(np.exp2(scales.astype(np.float64) - 127.0), 8, axis=1)[..., None]
    return vals.transpose(0, 1, 3, 2).reshape(g * 512, n)


def sigmoid(v):
    return 1.0 / (1.0 + np.exp(-v))


D, E, T, I, Q = 512, 512, 2048, 512, 128


def setup_inputs():
    n = np.random.standard_normal
    idx = np.random.permutation(T)[:I]
    fd = mx_kscale(D)
    fe = mx_kscale(E)
    keysp = pack_weight(n((D, T)) / fd[:, None], "e4m3")
    valsp = pack_weight(n((E, T)) / fe[:, None], "e4m3")
    return {
        "query": (n((D, Q)) * 0.5 / np.sqrt(D) * fd[:, None]).astype(np.float32),
        "query2": (n((D, Q)) * 0.8 / np.sqrt(D) * fd[:, None]).astype(np.float32),
        "keys_words": keysp[0],
        "keys_scales": keysp[1],
        "gout": (n((E, Q)) * 1 / np.sqrt(E) * fe[:, None]).astype(np.float32),
        "vals_words": valsp[0],
        "vals_scales": valsp[1],
        "size": (np.random.uniform(0.5, 2.0, (1, I))).astype(np.float32),
        "old": (0.5 * n((Q, T))).astype(np.float32),
        "offs": striped(idx),
    }


def reference(query, query2, keys_words, keys_scales, gout, vals_words, vals_scales, size, old, offs):
    idx = unstriped(offs)
    keysu = unpack_weight(keys_words, keys_scales, "e4m3")
    valsu = unpack_weight(vals_words, vals_scales, "e4m3")
    queryq = mxq(f64(query), 0, "e4m3")
    keysidxg = keysu[:, idx]
    a = queryq.T @ keysidxg
    query2q = mxq(f64(query2), 0, "e4m3")
    b = query2q.T @ keysidxg
    r = np.exp(a - np.max(a, axis=1, keepdims=True))
    gt = sigmoid(b)
    p = r * gt
    z = np.sum(p, axis=1, keepdims=True)
    goutq = mxq(f64(gout), 0, "e4m3")
    valsidxg = valsu[:, idx]
    c0 = goutq.T @ valsidxg
    dz = np.sum(c0 * p * f64(size) / np.square(z) * (-1.0), axis=1, keepdims=True)
    dp = c0 / z * f64(size) + dz
    dgt = dp * r
    db = dgt * gt * (1.0 - gt)
    gs = db * 512.0
    gf = np.zeros((Q, T))
    gf[:, idx] = gs
    y = f64(old) + gf
    return y

@@ -1,0 +1,149 @@
+from contextlib import ExitStack
+
+import concourse.mybir as mybir
+from concourse.masks import make_identity
+
+D, E, T, I, Q = 512, 512, 2048, 512, 128
+P = 128
+PACK = 4
+FLOPS = 3 * 2 * D * I * Q
+
+F32 = mybir.dt.float32
+BF16 = mybir.dt.bfloat16
+I32 = mybir.dt.int32
+U32 = mybir.dt.uint32
+U16 = mybir.dt.uint16
+U8 = mybir.dt.uint8
+FP8X4 = mybir.dt.float8_e4m3fn_x4
+ALU = mybir.AluOpType
+ACT = mybir.ActivationFunctionType
+AX = mybir.AxisListType
+
+STORE_WIDTHS = (256, 512, 512, 512, 256)
+
+
+def tile_attend_bgatedexp_b_s_kernel(tc, query, query2, keys_words, keys_scales, gout, vals_words, vals_scales, size, old, offs, out):
+    nc = tc.nc
+    with ExitStack() as ctx:
+        sb = ctx.enter_context(tc.tile_pool(name="sb", bufs=1))
+        ps = ctx.enter_context(tc.psum_pool(name="ps", bufs=1))
+
+        offsets = sb.tile([P, I // 16], U16, name="offsets")
+        nc.sync.dma_start(offsets[:], offs)
+
+        def load_words(words, name, tag):
+            pool_words = sb.tile([P, T], I32, name=name, tag=tag)
+            nc.sync.dma_start(pool_words[:], words[0].rearrange("p t r -> p (t r)").bitcast(I32))
+            return pool_words
+
+        def load_scales(scales, name, tag, clearer, queue):
+            plane = sb.tile([P, T // 4], I32, name=name, tag=tag)
+            clearer.memset(plane[:], 0)
+            rows = scales[0].bitcast(I32)
+            for quad in range(4):
+                queue.dma_start(plane[32 * quad : 32 * quad + 4, :], rows[4 * quad : 4 * quad + 4, :])
+            return plane
+
+        def load_rows(x, raw):
+            nc.sync.dma_start(raw[:], x.rearrange("(p j) q -> p j q", j=PACK))
+
+        def gather(src, dtype, name, tag):
+            got = sb.tile([P, I], dtype, name=name, tag=tag, align_bytes=64)
+            nc.vector.tensor_copy(got[:], src[:].bitcast(dtype).indirect(offsets[:]))
+            return got
+
+        def interleave(raw, name):
+            grouped = sb.tile([P, Q, PACK], BF16, name=name, tag=name, align_bytes=64)
+            nc.scalar.copy(
+                grouped[:].rearrange("p (c i) t -> p c t i", i=4),
+                raw[:].rearrange("p t (c i) -> p c t i", i=4),
+            )
+            return grouped
+
+        def quantize(grouped, name):
+            codes = sb.tile([P, Q], U32, name=name + "_codes", align_bytes=64)
+            scales = sb.tile([P, Q], U8, name=name + "_scales", align_bytes=64)
+            nc.vector.quantize_mx(out=codes[:].bitcast(FP8X4), scales=scales[:], in_=grouped[:].rearrange("p q t -> p (q t)"))
+            return codes, scales
+
+        def product(rows, words, scales, name):
+            acc = ps.tile([Q, I], F32, name=name, tag=name)
+            nc.tensor.matmul_mx(
+                out=acc[:], lhsT=rows[0][:].bitcast(FP8X4), lhsT_scale=rows[1][:],
+                rhs=words[:].bitcast(FP8X4), rhs_scale=scales[:], start=True, stop=True,
+            )
+            return acc
+
+        key_plane = load_scales(keys_scales, "key_plane", "plane_then_vals", nc.vector, nc.scalar)
+        key_pool = load_words(keys_words, "key_pool", "keys_then_old")
+        q2_raw = sb.tile([P, PACK, Q], F32, name="q2_raw")
+        q_raw = sb.tile([P, PACK, Q], F32, name="q_raw")
+        g_raw = sb.tile([P, PACK, Q], F32, name="g_raw")
+        load_rows(query2, q2_raw)
+        load_rows(query, q_raw)
+        val_plane = load_scales(vals_scales, "val_plane", "val_plane", nc.gpsimd, nc.gpsimd)
+        size_cols = sb.tile([P, 4], F32, name="size_cols")
+        nc.gpsimd.dma_start(size_cols[:], size.rearrange("o (p c) -> (o p) c", c=4))
+
+        window = sb.tile([Q, T], F32, name="window")
+        nc.vector.memset(window[:], 0.0)
+        nc.scalar.activation(g_raw[:, 0, 0:1], window[:, 0:1], ACT.Sigmoid)
+        load_rows(gout, g_raw)
+
+        ident = sb.tile([P, P], F32, name="ident")
+        make_identity(nc, ident[:])
+
+        key_scales = gather(key_plane, U8, "key_scales", "key_scales")
+        val_pool = load_words(vals_words, "val_pool", "plane_then_vals")
+        key_words = gather(key_pool, U32, "key_words", "key_words")
+        old_sb = sb.tile([Q, T], F32, name="old_sb", tag="keys_then_old")
+        nc.sync.dma_start(old_sb[:], old)
+        q2 = quantize(interleave(q2_raw, "q2_bf"), "q2")
+        b = product(q2, key_words, key_scales, "b")
+        q1 = quantize(interleave(q_raw, "q_bf"), "q1")
+        a = product(q1, key_words, key_scales, "a")
+        g_bf = interleave(g_raw, "g_bf")
+        gate = sb.tile([Q, I], F32, name="gate")
+        nc.scalar.activation(gate[:], b[:], ACT.Sigmoid)
+
+        size_ps = ps.tile([P, 4, P], F32, name="size_ps", tag="b")
+        for c in range(4):
+            nc.tensor.transpose(size_ps[:, c, :], size_cols[:, c : c + 1].to_broadcast([P, P]), ident[:])
+
+        val_scales = gather(val_plane, U8, "val_scales", "q_bf")
+        g = quantize(g_bf, "g")
+        neg_max = sb.tile([Q, 1], F32, name="neg_max")
+        nc.vector.tensor_reduce(neg_max[:], a[:], AX.X, ALU.max, negate=True)
+        r = sb.tile([Q, I], F32, name="r")
+        nc.scalar.activation(r[:], a[:], ACT.Exp, bias=neg_max[:])
+        size_row = sb.tile([P, P, 4], F32, name="size_row")
+        nc.scalar.copy(size_row[:], size_ps[:].rearrange("p c n -> p n c"))
+        rest = sb.tile([Q, I], F32, name="rest")
+        nc.scalar.activation(rest[:], gate[:], ACT.Identity, scale=-512.0, bias=512.0)
+
+        val_words = gather(val_pool, U32, "val_words", "val_words")
+        c0 = product(g, val_words, val_scales, "c0")
+
+        p = sb.tile([Q, I], F32, name="p")
+        z = sb.tile([Q, 1], F32, name="z")
+        nc.vector.scalar_tensor_tensor(p[:], r[:], 1.0, gate[:], ALU.mult, ALU.mult, accum_out=z[:])
+        cs = sb.tile([Q, I], F32, name="cs")
+        nc.vector.tensor_tensor(cs[:], c0[:], size_row[:].rearrange("p n c -> p (n c)"), ALU.mult)
+        rz = sb.tile([Q, 1], F32, name="rz")
+        nc.vector.reciprocal(rz[:], z[:])
+        factor = sb.tile([Q, I], F32, name="factor")
+        nc.scalar.activation(factor[:], rest[:], ACT.Copy, scale=rz[:])
+        weighted = sb.tile([Q, I], F32, name="weighted")
+        mean = sb.tile([Q, 1], F32, name="mean")
+        nc.vector.scalar_tensor_tensor(weighted[:], p[:], rz[:], cs[:], ALU.mult, ALU.mult, accum_out=mean[:])
+        u = sb.tile([Q, I], F32, name="u")
+        nc.vector.scalar_tensor_tensor(u[:], cs[:], mean[:], p[:], ALU.subtract, ALU.mult)
+        nc.vector.tensor_tensor(window[:].indirect(offsets[:]), u[:], factor[:], ALU.mult)
+
+        start = 0
+        for k, width in enumerate(STORE_WIDTHS):
+            cols = slice(start, start + width)
+            res = sb.tile([Q, width], F32, name="res%d" % k)
+            nc.vector.tensor_tensor(res[:], window[:, cols], old_sb[:, cols], ALU.add)
+            nc.sync.dma_start(out[:, cols], res[:])
+            start = start + width

@@ -32,20 +32,20 @@ def tile_attend_bgatedexp_b_s_kernel(tc, query, query2, keys_words, keys_scales,
         nc.sync.dma_start(offsets[:], offs)
 
         def load_words(words, name, tag):
-            pool_words = sb.tile([P, T], I32, name=name, tag=tag)
+            pool_words = sb.tile([P, T], I32, name=name, tag=tag, align_bytes=64)
             nc.sync.dma_start(pool_words[:], words[0].rearrange("p t r -> p (t r)").bitcast(I32))
             return pool_words
 
-        def load_scales(scales, name, tag, clearer, queue):
-            plane = sb.tile([P, T // 4], I32, name=name, tag=tag)
+        def load_scales(scales, name, tag, clearer, first):
+            plane = sb.tile([P, T // 4], I32, name=name, tag=tag, align_bytes=64)
             clearer.memset(plane[:], 0)
             rows = scales[0].bitcast(I32)
             for quad in range(4):
-                queue.dma_start(plane[32 * quad : 32 * quad + 4, :], rows[4 * quad : 4 * quad + 4, :])
+                nc.sync.dma_start(plane[32 * quad + first : 32 * quad + first + 4, :], rows[4 * quad : 4 * quad + 4, :])
             return plane
 
         def load_rows(x, raw):
-            nc.sync.dma_start(raw[:], x.rearrange("(p j) q -> p j q", j=PACK))
+            nc.sync.dma_start(raw, x.rearrange("(p j) q -> p j q", j=PACK))
 
         def gather(src, dtype, name, tag):
             got = sb.tile([P, I], dtype, name=name, tag=tag, align_bytes=64)
@@ -54,10 +54,7 @@ def tile_attend_bgatedexp_b_s_kernel(tc, query, query2, keys_words, keys_scales,
 
         def interleave(raw, name):
             grouped = sb.tile([P, Q, PACK], BF16, name=name, tag=name, align_bytes=64)
-            nc.scalar.copy(
-                grouped[:].rearrange("p (c i) t -> p c t i", i=4),
-                raw[:].rearrange("p t (c i) -> p c t i", i=4),
-            )
+            nc.scalar.copy(grouped[:], raw.rearrange("p t q -> p q t"))
             return grouped
 
         def quantize(grouped, name):
@@ -70,40 +67,42 @@ def tile_attend_bgatedexp_b_s_kernel(tc, query, query2, keys_words, keys_scales,
             acc = ps.tile([Q, I], F32, name=name, tag=name)
             nc.tensor.matmul_mx(
                 out=acc[:], lhsT=rows[0][:].bitcast(FP8X4), lhsT_scale=rows[1][:],
-                rhs=words[:].bitcast(FP8X4), rhs_scale=scales[:], start=True, stop=True,
+                rhs=words[:].bitcast(FP8X4), rhs_scale=scales, start=True, stop=True,
             )
             return acc
 
-        key_plane = load_scales(keys_scales, "key_plane", "plane_then_vals", nc.vector, nc.scalar)
-        key_pool = load_words(keys_words, "key_pool", "keys_then_old")
-        q2_raw = sb.tile([P, PACK, Q], F32, name="q2_raw")
-        q_raw = sb.tile([P, PACK, Q], F32, name="q_raw")
-        g_raw = sb.tile([P, PACK, Q], F32, name="g_raw")
-        load_rows(query2, q2_raw)
-        load_rows(query, q_raw)
-        val_plane = load_scales(vals_scales, "val_plane", "val_plane", nc.gpsimd, nc.gpsimd)
         size_cols = sb.tile([P, 4], F32, name="size_cols")
-        nc.gpsimd.dma_start(size_cols[:], size.rearrange("o (p c) -> (o p) c", c=4))
+        nc.scalar.dma_start(size_cols[:], size.rearrange("o (p c) -> (o p) c", c=4))
+        key_pool = load_words(keys_words, "key_pool", "pool")
+        key_plane = load_scales(keys_scales, "key_plane", "plane_then_old", nc.vector, 0)
+
+        staged = sb.tile([P, 3 * PACK * Q], F32, name="staged", tag="staged_then_gate")
+        raws = [staged[:, n * PACK * Q : (n + 1) * PACK * Q].rearrange("p (j q) -> p j q", j=PACK) for n in range(3)]
+        warm_in = sb.tile([P, 3], F32, name="warm_in")
+        warm_sum = sb.tile([P, 1], F32, name="warm_sum", tag="val_side", align_bytes=64)
+        nc.vector.memset(warm_in[:], 0.0)
+        nc.scalar.activation(staged[:, 0 : 3 * PACK * Q : PACK * Q], warm_in[:], ACT.Sigmoid, accum_out=warm_sum[:])
+        load_rows(query2, raws[0])
+        load_rows(query, raws[1])
+        load_rows(gout, raws[2])
+        val_plane = load_scales(vals_scales, "val_plane", "val_side", nc.vector, 4)
 
         window = sb.tile([Q, T], F32, name="window")
         nc.vector.memset(window[:], 0.0)
-        nc.scalar.activation(g_raw[:, 0, 0:1], window[:, 0:1], ACT.Sigmoid)
-        load_rows(gout, g_raw)
-
         ident = sb.tile([P, P], F32, name="ident")
         make_identity(nc, ident[:])
 
-        key_scales = gather(key_plane, U8, "key_scales", "key_scales")
-        val_pool = load_words(vals_words, "val_pool", "plane_then_vals")
         key_words = gather(key_pool, U32, "key_words", "key_words")
-        old_sb = sb.tile([Q, T], F32, name="old_sb", tag="keys_then_old")
+        val_pool = load_words(vals_words, "val_pool", "pool")
+        key_scales = gather(key_plane, U8, "key_scales", "key_scales")
+        old_sb = sb.tile([Q, T], F32, name="old_sb", tag="plane_then_old", align_bytes=64)
         nc.sync.dma_start(old_sb[:], old)
-        q2 = quantize(interleave(q2_raw, "q2_bf"), "q2")
-        b = product(q2, key_words, key_scales, "b")
-        q1 = quantize(interleave(q_raw, "q_bf"), "q1")
-        a = product(q1, key_words, key_scales, "a")
-        g_bf = interleave(g_raw, "g_bf")
-        gate = sb.tile([Q, I], F32, name="gate")
+        q2 = quantize(interleave(raws[0], "q2_bf"), "q2")
+        b = product(q2, key_words, key_scales[:], "b")
+        q1 = quantize(interleave(raws[1], "q_bf"), "q1")
+        a = product(q1, key_words, key_scales[:], "a")
+        g = quantize(interleave(raws[2], "g_bf"), "g")
+        gate = sb.tile([Q, I], F32, name="gate", tag="staged_then_gate")
         nc.scalar.activation(gate[:], b[:], ACT.Sigmoid)
 
         size_ps = ps.tile([P, 4, P], F32, name="size_ps", tag="b")
@@ -111,28 +110,28 @@ def tile_attend_bgatedexp_b_s_kernel(tc, query, query2, keys_words, keys_scales,
             nc.tensor.transpose(size_ps[:, c, :], size_cols[:, c : c + 1].to_broadcast([P, P]), ident[:])
 
         val_scales = gather(val_plane, U8, "val_scales", "q_bf")
-        g = quantize(g_bf, "g")
-        neg_max = sb.tile([Q, 1], F32, name="neg_max")
-        nc.vector.tensor_reduce(neg_max[:], a[:], AX.X, ALU.max, negate=True)
+        neg_max = sb.tile([Q, 1], F32, name="neg_max", tag="max_then_rest")
+        neg_a = sb.tile([Q, I], F32, name="neg_a", tag="val_side", align_bytes=64)
+        nc.vector.tensor_scalar(neg_a[:], a[:], -1.0, None, ALU.mult, ALU.min, accum_out=neg_max[:])
         r = sb.tile([Q, I], F32, name="r")
         nc.scalar.activation(r[:], a[:], ACT.Exp, bias=neg_max[:])
-        size_row = sb.tile([P, P, 4], F32, name="size_row")
-        nc.scalar.copy(size_row[:], size_ps[:].rearrange("p c n -> p n c"))
-        rest = sb.tile([Q, I], F32, name="rest")
-        nc.scalar.activation(rest[:], gate[:], ACT.Identity, scale=-512.0, bias=512.0)
+        rows = sb.tile([Q, 2 * I], F32, name="rows", tag="max_then_rest")
+        size_row, rest = rows[:, 0:I], rows[:, I : 2 * I]
+        nc.scalar.copy(size_row.rearrange("p (n c) -> p n c", c=4), size_ps[:].rearrange("p c n -> p n c"))
+        nc.scalar.activation(rest, gate[:], ACT.Identity, scale=-512.0, bias=512.0)
 
-        val_words = gather(val_pool, U32, "val_words", "val_words")
-        c0 = product(g, val_words, val_scales, "c0")
+        val_words = gather(val_pool, U32, "val_words", "val_side")
+        c0 = product(g, val_words, val_scales[4:P, :], "c0")
 
-        p = sb.tile([Q, I], F32, name="p")
+        p = sb.tile([Q, I], F32, name="p", tag="pool", align_bytes=64)
         z = sb.tile([Q, 1], F32, name="z")
         nc.vector.scalar_tensor_tensor(p[:], r[:], 1.0, gate[:], ALU.mult, ALU.mult, accum_out=z[:])
         cs = sb.tile([Q, I], F32, name="cs")
-        nc.vector.tensor_tensor(cs[:], c0[:], size_row[:].rearrange("p n c -> p (n c)"), ALU.mult)
+        nc.vector.tensor_tensor(cs[:], c0[:], size_row, ALU.mult)
         rz = sb.tile([Q, 1], F32, name="rz")
         nc.vector.reciprocal(rz[:], z[:])
         factor = sb.tile([Q, I], F32, name="factor")
-        nc.scalar.activation(factor[:], rest[:], ACT.Copy, scale=rz[:])
+        nc.scalar.activation(factor[:], rest, ACT.Copy, scale=rz[:])
         weighted = sb.tile([Q, I], F32, name="weighted")
         mean = sb.tile([Q, 1], F32, name="mean")
         nc.vector.scalar_tensor_tensor(weighted[:], p[:], rz[:], cs[:], ALU.mult, ALU.mult, accum_out=mean[:])

@@ -1,7 +1,6 @@
 from contextlib import ExitStack
 
 import concourse.mybir as mybir
-from concourse.masks import make_identity
 
 D, E, T, I, Q = 512, 512, 2048, 512, 128
 P = 128
@@ -52,29 +51,29 @@ def tile_attend_bgatedexp_b_s_kernel(tc, query, query2, keys_words, keys_scales,
             nc.vector.tensor_copy(got[:], src[:].bitcast(dtype).indirect(offsets[:]))
             return got
 
-        def interleave(raw, name):
-            grouped = sb.tile([P, Q, PACK], BF16, name=name, tag=name, align_bytes=64)
-            nc.scalar.copy(grouped[:], raw.rearrange("p t q -> p q t"))
-            return grouped
-
-        def quantize(grouped, name):
-            codes = sb.tile([P, Q], U32, name=name + "_codes", align_bytes=64)
-            scales = sb.tile([P, Q], U8, name=name + "_scales", align_bytes=64)
-            nc.vector.quantize_mx(out=codes[:].bitcast(FP8X4), scales=scales[:], in_=grouped[:].rearrange("p q t -> p (q t)"))
-            return codes, scales
+        def quantize(sources, name):
+            width = len(sources) * Q
+            grouped = sb.tile([P, width * PACK], BF16, name=name + "_bf", tag=name + "_bf", align_bytes=64)
+            for n, raw in enumerate(sources):
+                part = grouped[:, n * Q * PACK : (n + 1) * Q * PACK]
+                nc.scalar.copy(part.rearrange("p (q t) -> p q t", t=PACK), raw.rearrange("p t q -> p q t"))
+            codes = sb.tile([P, width], U32, name=name + "_codes", align_bytes=64)
+            scales = sb.tile([P, width], U8, name=name + "_scales", align_bytes=64)
+            nc.vector.quantize_mx(out=codes[:].bitcast(FP8X4), scales=scales[:], in_=grouped[:])
+            return [(codes[:, n * Q : (n + 1) * Q], scales[:, n * Q : (n + 1) * Q]) for n in range(len(sources))]
 
         def product(rows, words, scales, name):
             acc = ps.tile([Q, I], F32, name=name, tag=name)
             nc.tensor.matmul_mx(
-                out=acc[:], lhsT=rows[0][:].bitcast(FP8X4), lhsT_scale=rows[1][:],
+                out=acc[:], lhsT=rows[0].bitcast(FP8X4), lhsT_scale=rows[1],
                 rhs=words[:].bitcast(FP8X4), rhs_scale=scales, start=True, stop=True,
             )
             return acc
 
         size_cols = sb.tile([P, 4], F32, name="size_cols")
         nc.scalar.dma_start(size_cols[:], size.rearrange("o (p c) -> (o p) c", c=4))
-        key_pool = load_words(keys_words, "key_pool", "pool")
-        key_plane = load_scales(keys_scales, "key_plane", "plane_then_old", nc.vector, 0)
+        key_pool = load_words(keys_words, "key_pool", "key_pool")
+        key_plane = load_scales(keys_scales, "key_plane", "key_plane", nc.vector, 0)
 
         staged = sb.tile([P, 3 * PACK * Q], F32, name="staged", tag="staged_then_gate")
         raws = [staged[:, n * PACK * Q : (n + 1) * PACK * Q].rearrange("p (j q) -> p j q", j=PACK) for n in range(3)]
@@ -90,18 +89,19 @@ def tile_attend_bgatedexp_b_s_kernel(tc, query, query2, keys_words, keys_scales,
         window = sb.tile([Q, T], F32, name="window")
         nc.vector.memset(window[:], 0.0)
         ident = sb.tile([P, P], F32, name="ident")
-        make_identity(nc, ident[:])
+        zeros = sb.tile([P, P], F32, name="zeros", tag="pool", align_bytes=64)
+        nc.gpsimd.memset(zeros[:], 0.0)
+        nc.gpsimd.affine_select(
+            out=ident[:], in_=zeros[:], pattern=[[-1, P]], compare_op=ALU.not_equal, fill=1.0, base=0, channel_multiplier=1
+        )
+        val_pool = load_words(vals_words, "val_pool", "pool")
 
         key_words = gather(key_pool, U32, "key_words", "key_words")
-        val_pool = load_words(vals_words, "val_pool", "pool")
         key_scales = gather(key_plane, U8, "key_scales", "key_scales")
-        old_sb = sb.tile([Q, T], F32, name="old_sb", tag="plane_then_old", align_bytes=64)
-        nc.sync.dma_start(old_sb[:], old)
-        q2 = quantize(interleave(raws[0], "q2_bf"), "q2")
+        (q2,) = quantize(raws[0:1], "q2")
         b = product(q2, key_words, key_scales[:], "b")
-        q1 = quantize(interleave(raws[1], "q_bf"), "q1")
+        q1, g = quantize(raws[1:3], "qg")
         a = product(q1, key_words, key_scales[:], "a")
-        g = quantize(interleave(raws[2], "g_bf"), "g")
         gate = sb.tile([Q, I], F32, name="gate", tag="staged_then_gate")
         nc.scalar.activation(gate[:], b[:], ACT.Sigmoid)
 
@@ -109,7 +109,7 @@ def tile_attend_bgatedexp_b_s_kernel(tc, query, query2, keys_words, keys_scales,
         for c in range(4):
             nc.tensor.transpose(size_ps[:, c, :], size_cols[:, c : c + 1].to_broadcast([P, P]), ident[:])
 
-        val_scales = gather(val_plane, U8, "val_scales", "q_bf")
+        val_scales = gather(val_plane, U8, "val_scales", "qg_bf")
         neg_max = sb.tile([Q, 1], F32, name="neg_max", tag="max_then_rest")
         neg_a = sb.tile([Q, I], F32, name="neg_a", tag="val_side", align_bytes=64)
         nc.vector.tensor_scalar(neg_a[:], a[:], -1.0, None, ALU.mult, ALU.min, accum_out=neg_max[:])
@@ -123,9 +123,11 @@ def tile_attend_bgatedexp_b_s_kernel(tc, query, query2, keys_words, keys_scales,
         val_words = gather(val_pool, U32, "val_words", "val_side")
         c0 = product(g, val_words, val_scales[4:P, :], "c0")
 
-        p = sb.tile([Q, I], F32, name="p", tag="pool", align_bytes=64)
+        last = sb.tile([Q, I + T], F32, name="last", tag="pool", align_bytes=64)
+        p, old_sb = last[:, 0:I], last[:, I : I + T]
+        nc.sync.dma_start(old_sb, old)
         z = sb.tile([Q, 1], F32, name="z")
-        nc.vector.scalar_tensor_tensor(p[:], r[:], 1.0, gate[:], ALU.mult, ALU.mult, accum_out=z[:])
+        nc.vector.scalar_tensor_tensor(p, r[:], 1.0, gate[:], ALU.mult, ALU.mult, accum_out=z[:])
         cs = sb.tile([Q, I], F32, name="cs")
         nc.vector.tensor_tensor(cs[:], c0[:], size_row, ALU.mult)
         rz = sb.tile([Q, 1], F32, name="rz")
@@ -134,9 +136,9 @@ def tile_attend_bgatedexp_b_s_kernel(tc, query, query2, keys_words, keys_scales,
         nc.scalar.activation(factor[:], rest, ACT.Copy, scale=rz[:])
         weighted = sb.tile([Q, I], F32, name="weighted")
         mean = sb.tile([Q, 1], F32, name="mean")
-        nc.vector.scalar_tensor_tensor(weighted[:], p[:], rz[:], cs[:], ALU.mult, ALU.mult, accum_out=mean[:])
+        nc.vector.scalar_tensor_tensor(weighted[:], p, rz[:], cs[:], ALU.mult, ALU.mult, accum_out=mean[:])
         u = sb.tile([Q, I], F32, name="u")
-        nc.vector.scalar_tensor_tensor(u[:], cs[:], mean[:], p[:], ALU.subtract, ALU.mult)
+        nc.vector.scalar_tensor_tensor(u[:], cs[:], mean[:], p, ALU.subtract, ALU.mult)
         nc.vector.tensor_tensor(window[:].indirect(offsets[:]), u[:], factor[:], ALU.mult)
 
         start = 0

@@ -72,35 +72,39 @@ def tile_attend_bgatedexp_b_s_kernel(tc, query, query2, keys_words, keys_scales,
 
         size_cols = sb.tile([P, 4], F32, name="size_cols")
         nc.scalar.dma_start(size_cols[:], size.rearrange("o (p c) -> (o p) c", c=4))
-        key_pool = load_words(keys_words, "key_pool", "key_pool")
+        q2_raw = sb.tile([P, PACK, Q], F32, name="q2_raw")
+        load_rows(query2, q2_raw[:])
         key_plane = load_scales(keys_scales, "key_plane", "key_plane", nc.vector, 0)
 
-        staged = sb.tile([P, 3 * PACK * Q], F32, name="staged", tag="staged_then_gate")
-        raws = [staged[:, n * PACK * Q : (n + 1) * PACK * Q].rearrange("p (j q) -> p j q", j=PACK) for n in range(3)]
-        warm_in = sb.tile([P, 3], F32, name="warm_in")
-        warm_sum = sb.tile([P, 1], F32, name="warm_sum", tag="val_side", align_bytes=64)
-        nc.vector.memset(warm_in[:], 0.0)
-        nc.scalar.activation(staged[:, 0 : 3 * PACK * Q : PACK * Q], warm_in[:], ACT.Sigmoid, accum_out=warm_sum[:])
-        load_rows(query2, raws[0])
-        load_rows(query, raws[1])
-        load_rows(gout, raws[2])
-        val_plane = load_scales(vals_scales, "val_plane", "val_side", nc.vector, 4)
-
-        window = sb.tile([Q, T], F32, name="window")
-        nc.vector.memset(window[:], 0.0)
         ident = sb.tile([P, P], F32, name="ident")
         zeros = sb.tile([P, P], F32, name="zeros", tag="pool", align_bytes=64)
         nc.gpsimd.memset(zeros[:], 0.0)
         nc.gpsimd.affine_select(
             out=ident[:], in_=zeros[:], pattern=[[-1, P]], compare_op=ALU.not_equal, fill=1.0, base=0, channel_multiplier=1
         )
-        val_pool = load_words(vals_words, "val_pool", "pool")
+        key_pool = load_words(keys_words, "key_pool", "pool")
 
-        key_words = gather(key_pool, U32, "key_words", "key_words")
+        staged = sb.tile([P, 2 * PACK * Q], F32, name="staged", tag="staged_then_gate")
+        raws = [staged[:, n * PACK * Q : (n + 1) * PACK * Q].rearrange("p (j q) -> p j q", j=PACK) for n in range(2)]
+        warm_bias = sb.tile([P, 1], F32, name="warm_bias", tag="q2_bf", align_bytes=64)
+        warm_sum = sb.tile([P, 1], F32, name="warm_sum", tag="val_side", align_bytes=64)
+        nc.vector.memset(warm_bias[:], 0.0)
+        nc.scalar.activation(staged[:, 0 : 2 * PACK * Q : PACK * Q], ident[:, 0:2], ACT.Sigmoid, bias=warm_bias[:], accum_out=warm_sum[:])
+        load_rows(query, raws[0])
+        load_rows(gout, raws[1])
+        val_plane = load_scales(vals_scales, "val_plane", "val_side", nc.vector, 4)
+
+        window = sb.tile([Q, T], F32, name="window")
+        nc.vector.memset(window[:], 0.0)
+
         key_scales = gather(key_plane, U8, "key_scales", "key_scales")
-        (q2,) = quantize(raws[0:1], "q2")
+        (q2,) = quantize([q2_raw[:]], "q2")
+        val_pool = load_words(vals_words, "val_pool", "q2_bf")
+        key_words = gather(key_pool, U32, "key_words", "key_words")
+        old_sb = sb.tile([Q, T], F32, name="old_sb", tag="pool", align_bytes=64)
+        nc.sync.dma_start(old_sb[:], old)
         b = product(q2, key_words, key_scales[:], "b")
-        q1, g = quantize(raws[1:3], "qg")
+        q1, g = quantize(raws, "qg")
         a = product(q1, key_words, key_scales[:], "a")
         gate = sb.tile([Q, I], F32, name="gate", tag="staged_then_gate")
         nc.scalar.activation(gate[:], b[:], ACT.Sigmoid)
@@ -123,9 +127,8 @@ def tile_attend_bgatedexp_b_s_kernel(tc, query, query2, keys_words, keys_scales,
         val_words = gather(val_pool, U32, "val_words", "val_side")
         c0 = product(g, val_words, val_scales[4:P, :], "c0")
 
-        last = sb.tile([Q, I + T], F32, name="last", tag="pool", align_bytes=64)
-        p, old_sb = last[:, 0:I], last[:, I : I + T]
-        nc.sync.dma_start(old_sb, old)
+        p_tile = sb.tile([Q, I], F32, name="p_tile", tag="q2_bf", align_bytes=64)
+        p = p_tile[:]
         z = sb.tile([Q, 1], F32, name="z")
         nc.vector.scalar_tensor_tensor(p, r[:], 1.0, gate[:], ALU.mult, ALU.mult, accum_out=z[:])
         cs = sb.tile([Q, I], F32, name="cs")

from contextlib import ExitStack

import concourse.mybir as mybir

D, E, T, I, Q = 512, 512, 2048, 512, 128
P = 128
PACK = 4
FLOPS = 3 * 2 * D * I * Q

F32 = mybir.dt.float32
BF16 = mybir.dt.bfloat16
I32 = mybir.dt.int32
U32 = mybir.dt.uint32
U16 = mybir.dt.uint16
U8 = mybir.dt.uint8
FP8X4 = mybir.dt.float8_e4m3fn_x4
ALU = mybir.AluOpType
ACT = mybir.ActivationFunctionType
AX = mybir.AxisListType

STORE_WIDTHS = (256, 512, 512, 512, 256)


def tile_attend_bgatedexp_b_s_kernel(tc, query, query2, keys_words, keys_scales, gout, vals_words, vals_scales, size, old, offs, out):
    nc = tc.nc
    with ExitStack() as ctx:
        sb = ctx.enter_context(tc.tile_pool(name="sb", bufs=1))
        ps = ctx.enter_context(tc.psum_pool(name="ps", bufs=1))

        offsets = sb.tile([P, I // 16], U16, name="offsets")
        nc.sync.dma_start(offsets[:], offs)

        def load_words(words, name, tag):
            pool_words = sb.tile([P, T], I32, name=name, tag=tag, align_bytes=64)
            nc.sync.dma_start(pool_words[:], words[0].rearrange("p t r -> p (t r)").bitcast(I32))
            return pool_words

        def load_scales(scales, name, tag, clearer, first):
            plane = sb.tile([P, T // 4], I32, name=name, tag=tag, align_bytes=64)
            clearer.memset(plane[:], 0)
            rows = scales[0].bitcast(I32)
            for quad in range(4):
                nc.sync.dma_start(plane[32 * quad + first : 32 * quad + first + 4, :], rows[4 * quad : 4 * quad + 4, :])
            return plane

        def load_rows(x, raw):
            nc.sync.dma_start(raw, x.rearrange("(p j) q -> p j q", j=PACK))

        def gather(src, dtype, name, tag):
            got = sb.tile([P, I], dtype, name=name, tag=tag, align_bytes=64)
            nc.vector.tensor_copy(got[:], src[:].bitcast(dtype).indirect(offsets[:]))
            return got

        def quantize(sources, name):
            width = len(sources) * Q
            grouped = sb.tile([P, width * PACK], BF16, name=name + "_bf", tag=name + "_bf", align_bytes=64)
            for n, raw in enumerate(sources):
                part = grouped[:, n * Q * PACK : (n + 1) * Q * PACK]
                nc.scalar.copy(part.rearrange("p (q t) -> p q t", t=PACK), raw.rearrange("p t q -> p q t"))
            codes = sb.tile([P, width], U32, name=name + "_codes", align_bytes=64)
            scales = sb.tile([P, width], U8, name=name + "_scales", align_bytes=64)
            nc.vector.quantize_mx(out=codes[:].bitcast(FP8X4), scales=scales[:], in_=grouped[:])
            return [(codes[:, n * Q : (n + 1) * Q], scales[:, n * Q : (n + 1) * Q]) for n in range(len(sources))]

        def product(rows, words, scales, name):
            acc = ps.tile([Q, I], F32, name=name, tag=name)
            nc.tensor.matmul_mx(
                out=acc[:], lhsT=rows[0].bitcast(FP8X4), lhsT_scale=rows[1],
                rhs=words[:].bitcast(FP8X4), rhs_scale=scales, start=True, stop=True,
            )
            return acc

        size_cols = sb.tile([P, 4], F32, name="size_cols")
        nc.scalar.dma_start(size_cols[:], size.rearrange("o (p c) -> (o p) c", c=4))
        q2_raw = sb.tile([P, PACK, Q], F32, name="q2_raw")
        load_rows(query2, q2_raw[:])
        key_plane = load_scales(keys_scales, "key_plane", "key_plane", nc.vector, 0)

        ident = sb.tile([P, P], F32, name="ident")
        zeros = sb.tile([P, P], F32, name="zeros", tag="pool", align_bytes=64)
        nc.gpsimd.memset(zeros[:], 0.0)
        nc.gpsimd.affine_select(
            out=ident[:], in_=zeros[:], pattern=[[-1, P]], compare_op=ALU.not_equal, fill=1.0, base=0, channel_multiplier=1
        )
        key_pool = load_words(keys_words, "key_pool", "pool")

        staged = sb.tile([P, 2 * PACK * Q], F32, name="staged", tag="staged_then_gate")
        raws = [staged[:, n * PACK * Q : (n + 1) * PACK * Q].rearrange("p (j q) -> p j q", j=PACK) for n in range(2)]
        warm_bias = sb.tile([P, 1], F32, name="warm_bias", tag="q2_bf", align_bytes=64)
        warm_sum = sb.tile([P, 1], F32, name="warm_sum", tag="val_side", align_bytes=64)
        nc.vector.memset(warm_bias[:], 0.0)
        nc.scalar.activation(staged[:, 0 : 2 * PACK * Q : PACK * Q], ident[:, 0:2], ACT.Sigmoid, bias=warm_bias[:], accum_out=warm_sum[:])
        load_rows(query, raws[0])
        load_rows(gout, raws[1])
        val_plane = load_scales(vals_scales, "val_plane", "val_side", nc.vector, 4)

        window = sb.tile([Q, T], F32, name="window")
        nc.vector.memset(window[:], 0.0)

        key_scales = gather(key_plane, U8, "key_scales", "key_scales")
        (q2,) = quantize([q2_raw[:]], "q2")
        val_pool = load_words(vals_words, "val_pool", "q2_bf")
        key_words = gather(key_pool, U32, "key_words", "key_words")
        old_sb = sb.tile([Q, T], F32, name="old_sb", tag="pool", align_bytes=64)
        nc.sync.dma_start(old_sb[:], old)
        b = product(q2, key_words, key_scales[:], "b")
        q1, g = quantize(raws, "qg")
        a = product(q1, key_words, key_scales[:], "a")
        gate = sb.tile([Q, I], F32, name="gate", tag="staged_then_gate")
        nc.scalar.activation(gate[:], b[:], ACT.Sigmoid)

        size_ps = ps.tile([P, 4, P], F32, name="size_ps", tag="b")
        for c in range(4):
            nc.tensor.transpose(size_ps[:, c, :], size_cols[:, c : c + 1].to_broadcast([P, P]), ident[:])

        val_scales = gather(val_plane, U8, "val_scales", "qg_bf")
        neg_max = sb.tile([Q, 1], F32, name="neg_max", tag="max_then_rest")
        neg_a = sb.tile([Q, I], F32, name="neg_a", tag="val_side", align_bytes=64)
        nc.vector.tensor_scalar(neg_a[:], a[:], -1.0, None, ALU.mult, ALU.min, accum_out=neg_max[:])
        r = sb.tile([Q, I], F32, name="r")
        nc.scalar.activation(r[:], a[:], ACT.Exp, bias=neg_max[:])
        rows = sb.tile([Q, 2 * I], F32, name="rows", tag="max_then_rest")
        size_row, rest = rows[:, 0:I], rows[:, I : 2 * I]
        nc.scalar.copy(size_row.rearrange("p (n c) -> p n c", c=4), size_ps[:].rearrange("p c n -> p n c"))
        nc.scalar.activation(rest, gate[:], ACT.Identity, scale=-512.0, bias=512.0)

        val_words = gather(val_pool, U32, "val_words", "val_side")
        c0 = product(g, val_words, val_scales[4:P, :], "c0")

        p_tile = sb.tile([Q, I], F32, name="p_tile", tag="q2_bf", align_bytes=64)
        p = p_tile[:]
        z = sb.tile([Q, 1], F32, name="z")
        nc.vector.scalar_tensor_tensor(p, r[:], 1.0, gate[:], ALU.mult, ALU.mult, accum_out=z[:])
        cs = sb.tile([Q, I], F32, name="cs")
        nc.vector.tensor_tensor(cs[:], c0[:], size_row, ALU.mult)
        rz = sb.tile([Q, 1], F32, name="rz")
        nc.vector.reciprocal(rz[:], z[:])
        factor = sb.tile([Q, I], F32, name="factor")
        nc.scalar.activation(factor[:], rest, ACT.Copy, scale=rz[:])
        weighted = sb.tile([Q, I], F32, name="weighted")
        mean = sb.tile([Q, 1], F32, name="mean")
        nc.vector.scalar_tensor_tensor(weighted[:], p, rz[:], cs[:], ALU.mult, ALU.mult, accum_out=mean[:])
        u = sb.tile([Q, I], F32, name="u")
        nc.vector.scalar_tensor_tensor(u[:], cs[:], mean[:], p, ALU.subtract, ALU.mult)
        nc.vector.tensor_tensor(window[:].indirect(offsets[:]), u[:], factor[:], ALU.mult)

        start = 0
        for k, width in enumerate(STORE_WIDTHS):
            cols = slice(start, start + width)
            res = sb.tile([Q, width], F32, name="res%d" % k)
            nc.vector.tensor_tensor(res[:], window[:, cols], old_sb[:, cols], ALU.add)
            nc.sync.dma_start(out[:, cols], res[:])
            start = start + width
